import numpy as np
import ml_dtypes


def mxq(x, axis, fmt="e4m3"):
    dtype, down = {"e4m3": (ml_dtypes.float8_e4m3fn, 7), "e5m2": (ml_dtypes.float8_e5m2, 14)}[fmt]
    v = np.moveaxis(np.asarray(x, np.float32).astype(ml_dtypes.bfloat16).astype(np.float64), axis, -1)
    blocks = v.reshape(v.shape[:-1] + (-1, 32))
    amax = np.abs(blocks).max(-1, keepdims=True)
    byte = np.maximum(np.where(amax > 0, np.frexp(amax)[1] - 1 + 127, 0) - down, 1)
    scale = np.exp2(byte - 127.0)
    codes = (blocks / scale).astype(np.float32).astype(dtype).astype(np.float64)
    return np.moveaxis((codes * scale).reshape(v.shape), -1, axis)


WIDE = False


def mx_kscale(k):
    if not WIDE:
        return np.ones(k)
    levels = np.array([24, -24, 12, -12, 0])
    if k % 512:
        return np.exp2(np.random.permutation(np.resize(levels, k // 32))).repeat(32)
    a = np.empty((k // 512, 16))
    for p in range(k // 512):
        a[p, :8] = np.random.permutation(np.resize(levels, 8))
        for g in range(8):
            far = levels[np.abs(levels - a[p, g]) >= 10]
            a[p, g + 8] = far[np.random.randint(len(far))]
    return np.exp2(a.ravel()).repeat(32)


def f64(x):
    return np.asarray(x).astype(np.float64)


def striped(idx):
    return np.tile(idx.reshape(-1, 16).T, (8, 1)).astype(np.uint16)


def unstriped(offs):
    return offs[:16].T.reshape(-1).astype(np.int64)


E2M1 = np.array([0.0, 0.5, 1.0, 1.5, 2.0, 3.0, 4.0, 6.0, -0.0, -0.5, -1.0, -1.5, -2.0, -3.0, -4.0, -6.0])


def pack_weight(w, fmt):
    k, n = w.shape
    w = f64(np.asarray(w, np.float32).astype(ml_dtypes.bfloat16)).reshape(k // 32, 32, n)
    amax = np.abs(w).max(1)
    if fmt == "e4m3":
        byte = np.frexp(amax)[1] - 1 + 127 - 7
    else:
        mant, ex = np.frexp(amax / 6.0)
        byte = np.where(mant > 0.5, ex, ex - 1) + 127
    byte = np.clip(np.where(amax > 0, byte, 1), 1, 254)
    scaled = (w * np.exp2(127.0 - byte)[:, None, :]).reshape(k, n).astype(np.float32)
    by_word = np.ascontiguousarray(scaled.reshape(k // 512, 128, 4, n).transpose(0, 1, 3, 2))
    if fmt == "e4m3":
        words = by_word.astype(ml_dtypes.float8_e4m3fn).view(np.uint8)
    else:
        c = by_word.astype(ml_dtypes.float4_e2m1fn).view(np.uint8) & 0xF
        words = (c[..., 0::2] | (c[..., 1::2] << 4)).reshape(k // 512, 128, 2 * n)
    return np.ascontiguousarray(words), np.ascontiguousarray(byte.astype(np.uint8).reshape(k // 512, 16, n))


def unpack_weight(words, scales, fmt):
    g, _, n = scales.shape
    words = np.ascontiguousarray(words).reshape(g, 128, n, -1)
    if fmt == "e4m3":
        vals = words.view(ml_dtypes.float8_e4m3fn).astype(np.float64)
    else:
        nib = np.empty((g, 128, n, 4), np.uint8)
        nib[..., 0::2] = words & 0xF
        nib[..., 1::2] = words >> 4
        vals = E2M1[nib]
    vals = vals * np.repeat(np.exp2(scales.astype(np.float64) - 127.0), 8, axis=1)[..., None]
    return vals.transpose(0, 1, 3, 2).reshape(g * 512, n)


def pack_table4(v):
    words, scales = pack_weight(v, "e2m1")
    g, t = words.shape[0] // 2, v.shape[1]
    return np.ascontiguousarray(words.reshape(g, 2, 128, t, 2).transpose(0, 2, 3, 1, 4).reshape(g, 128, t, 4)), scales


def unpack_table4(words, scales):
    g, _, t, _ = words.shape
    return unpack_weight(words.reshape(g, 128, t, 2, 2).transpose(0, 3, 1, 2, 4).reshape(2 * g, 128, 2 * t), scales, "e2m1")


def planes(y):
    n, m = y.shape
    v = y.astype(np.float32).astype(ml_dtypes.bfloat16).astype(np.float64).reshape(n // 32, 32, m)
    top = np.abs(v).max(1)
    byte = np.clip(np.where(top > 0, np.frexp(top)[1] - 1 + 127 - 7, 1), 1, 254)
    codes = (v * np.exp2(127.0 - byte)[:, None, :]).reshape(n, m).astype(np.float32).astype(ml_dtypes.float8_e4m3fn).view(np.uint8)
    words = codes.reshape(n // 512, 128, 4, m).transpose(0, 1, 3, 2)
    return np.ascontiguousarray(words), np.ascontiguousarray(byte.astype(np.uint8).reshape(n // 512, 16, m))


def sigm(f):
    return 1.0 / (1.0 + np.exp(-np.maximum(f, -700.0)))


K, N, T, J = 1024, 512, 2048, 1024


def setup_inputs():
    n = np.random.standard_normal
    s = mx_kscale(K)[:, None]
    p_tab = pack_table4(n((K, T)) * s)
    p_wa = pack_weight(n((K, N)) / np.sqrt(2 * K) / s, "e2m1")
    p_wc = pack_weight(n((K, N)) / np.sqrt(K) / s, "e2m1")
    return {
        "tab_words": p_tab[0],
        "tab_scales": p_tab[1],
        "wa_words": p_wa[0],
        "wa_scales": p_wa[1],
        "wb": (n((K, N)) / np.sqrt(2 * K) / s).astype(np.float32),
        "wc_words": p_wc[0],
        "wc_scales": p_wc[1],
        "wo": (n((K, N)) / np.sqrt(K) / s).astype(np.float32),
        "wgo": np.tile(np.random.uniform(0.5, 2.0, J), (128, 1)).astype(np.float32),
        "offs": striped(np.random.permutation(T)[:J]),
        "offs2": striped(np.random.permutation(T)[:J]),
    }


def reference(tab_words, tab_scales, wa_words, wa_scales, wb, wc_words, wc_scales, wo, wgo, offs, offs2):
    idx = unstriped(offs)
    idx2 = unstriped(offs2)
    tab_ = unpack_table4(tab_words, tab_scales)[:, idx]
    tabb_ = unpack_table4(tab_words, tab_scales)[:, idx2]
    wa_ = unpack_weight(wa_words, wa_scales, "e2m1")
    wb_ = mxq(f64(wb), 0, "e4m3")
    za = wa_.T @ tabb_ + wb_.T @ tab_
    eta = sigm(za)
    wc_ = unpack_weight(wc_words, wc_scales, "e2m1")
    ms = wc_.T @ tab_
    wo_ = mxq(f64(wo), 0, "e4m3")
    ow = wo_.T @ tabb_
    out = np.zeros((N, T))
    out[:, idx2] = f64(wgo)[0] * (np.maximum(ow + eta * ms, 0.0))
    return (out,) + planes(out)

@@ -1,0 +1,308 @@
+from contextlib import ExitStack
+
+import concourse.mybir as mybir
+from concourse.masks import make_identity
+
+K, N, T, J = 1024, 512, 2048, 1024
+FLOPS = 4 * 2 * K * N * J
+
+F32 = mybir.dt.float32
+BF16 = mybir.dt.bfloat16
+I32 = mybir.dt.int32
+U32 = mybir.dt.uint32
+U16 = mybir.dt.uint16
+U8 = mybir.dt.uint8
+FP8X4 = mybir.dt.float8_e4m3fn_x4
+FP4X4 = mybir.dt.float4_e2m1fn_x4
+ACT = mybir.ActivationFunctionType
+MULT = mybir.AluOpType.mult
+
+P = 128
+PACK = 4
+PASSES = K // (P * PACK)
+BLOCK = 128
+BLOCKS = J // BLOCK
+HALF = J // 2
+CHUNK = 256
+CHUNKS = T // CHUNK
+
+
+def tile_list_rgg_ownreluP_kernel(
+    tc, tab_words, tab_scales, wa_words, wa_scales, wb, wc_words, wc_scales, wo, wgo, offs, offs2, out_0, out_1, out_2
+):
+    nc = tc.nc
+    with ExitStack() as ctx:
+        keep = ctx.enter_context(tc.tile_pool(name="keep", bufs=1))
+        ring = ctx.enter_context(tc.tile_pool(name="ring", bufs=2))
+        psum = ctx.enter_context(tc.psum_pool(name="psum", bufs=1))
+
+        def held(shape, dtype, name, tag=""):
+            return keep.tile(shape, dtype, name=name, tag=tag or name, align_bytes=64)
+
+        src_list = keep.tile([P, J // 16], U16, name="src_list")
+        dst_list = keep.tile([P, J // 16], U16, name="dst_list")
+        nc.sync.dma_start(src_list[:], offs)
+        nc.sync.dma_start(dst_list[:], offs2)
+        lists = {"src": src_list, "dst": dst_list}
+
+        table_scales = held([P, T], U8, "table_scales")
+        nc.gpsimd.memset(table_scales[:].bitcast(I32), 0)
+        table_words = held([P, T], I32, "table_words")
+        nc.sync.dma_start(table_words[:], tab_words[0].rearrange("p t b -> p (t b)").bitcast(I32))
+        scale_rows = tab_scales.rearrange("a (q r) t -> r q a t", r=4)
+        for r in range(4):
+            nc.sync.dma_start(table_scales[r:P:16, :].bitcast(I32), scale_rows[r].bitcast(I32))
+
+        warm = held([P, 1], F32, "warm")
+        nc.gpsimd.memset(warm[:], 0.0)
+        warm_out = held([P, 1], F32, "warm_out")
+        nc.scalar.activation(warm_out[:], warm[:], ACT.Sigmoid)
+
+        packed_words, packed_scales = {}, {}
+        for name in ("wa", "wc"):
+            packed_words[name] = held([P, PASSES * 2 * N], U8, name + "_words")
+            packed_scales[name] = held([P, PASSES * N], U8, name + "_scales")
+            nc.gpsimd.memset(packed_scales[name][:].bitcast(I32), 0)
+        moved_scales = {}
+        for h in range(2):
+            for name in ("dst", "src"):
+                moved_scales[name, h] = held([P, HALF], U8, "%s_moved_scales%d" % (name, h))
+                nc.gpsimd.memset(moved_scales[name, h][:].bitcast(I32), 0)
+        identity = held([P, P], F32, "identity")
+        make_identity(nc, identity[:])
+
+        def load_packed_words(name, words):
+            nc.sync.dma_start(
+                packed_words[name][:].bitcast(I32).rearrange("p (a c) -> p a c", a=PASSES),
+                words.rearrange("a p c -> p a c").bitcast(I32),
+            )
+
+        def load_packed_scales(name, scales):
+            rows = scales.rearrange("a (q r) n -> r q a n", r=4)
+            for r in range(4):
+                nc.sync.dma_start(
+                    packed_scales[name][r:P:32, :].bitcast(I32).rearrange("q (a c) -> q a c", a=PASSES),
+                    rows[r].bitcast(I32),
+                )
+
+        raw = {}
+
+        def load_raw(name, w, a, first, last):
+            raw[name, a, first] = held([P, PACK, last - first], F32, "%s_raw%d_%d" % (name, a, first))
+            rows = w[a * P * PACK : (a + 1) * P * PACK, first:last]
+            nc.sync.dma_start(raw[name, a, first][:], rows.rearrange("(p i) n -> p i n", i=PACK))
+
+        load_raw("wb", wb, 0, 0, N)
+        load_raw("wb", wb, 1, 0, N)
+        load_packed_words("wa", wa_words)
+        load_packed_scales("wa", wa_scales)
+        load_packed_words("wc", wc_words)
+        load_raw("wo", wo, 0, 0, N)
+        load_packed_scales("wc", wc_scales)
+        load_raw("wo", wo, 1, 0, N // 2)
+        load_raw("wo", wo, 1, N // 2, N)
+
+        pages = [held([P, T], F32, "page%d" % t) for t in range(PACK)]
+        for t in range(PACK):
+            engine = nc.vector if t < 2 else nc.gpsimd
+            engine.memset(pages[t][:].bitcast(I32), 0)
+
+        picked_scales = {}
+
+        def pick_scales(h):
+            cols = slice(h * HALF // 16, (h + 1) * HALF // 16)
+            for name in ("dst", "src"):
+                after = {("dst", 1): "wb_grouped0_0", ("src", 1): "wb_grouped1_0"}.get((name, h), "")
+                picked_scales[name, h] = held([P, HALF], U8, "%s_picked_scales%d" % (name, h), after)
+                nc.vector.tensor_copy(picked_scales[name, h][:], table_scales[:].indirect(lists[name][:, cols]))
+                nc.gpsimd.dma_start(
+                    moved_scales[name, h][0 : P - 16, :].bitcast(I32), picked_scales[name, h][16:P, :].bitcast(I32)
+                )
+
+        parted = {}
+
+        def pick_words(first, last, after):
+            picked = {}
+            width = last - first
+            for name in ("dst", "src"):
+                picked[name] = held([P, width], U32, "%s_picked%d" % (name, first), after.get(name, ""))
+                nc.vector.tensor_copy(
+                    picked[name][:], table_words[:].bitcast(U32).indirect(lists[name][:, first // 16 : last // 16])
+                )
+            for name in ("dst", "src"):
+                words = held([P, PASSES * 2 * width], U8, "%s_parted%d" % (name, first))
+                nc.vector.tensor_copy(
+                    words[:].bitcast(U16).rearrange("p (a j) -> p a j", a=PASSES),
+                    picked[name][:].bitcast(U16).rearrange("p (j a) -> p a j", a=PASSES),
+                )
+                for b in range(first // BLOCK, last // BLOCK):
+                    at = b * BLOCK - first
+                    for a in range(PASSES):
+                        parted[name, a, b] = words[:, 2 * (a * width + at) : 2 * (a * width + at + BLOCK)]
+
+        codes, planes = {}, {}
+
+        def quantize_weight(name, a, parts):
+            codes[name, a] = held([P, N], U32, "%s_codes%d" % (name, a))
+            planes[name, a] = held([P, N], U8, "%s_plane%d" % (name, a))
+            for first, last, copy in parts:
+                grouped = held([P, (last - first) * PACK], BF16, "%s_grouped%d_%d" % (name, a, first))
+                copy(
+                    grouped[:].rearrange("p (c m i) -> p c i m", m=4, i=PACK),
+                    raw[name, a, first][:].rearrange("p i (c m) -> p c i m", m=4),
+                )
+                nc.vector.quantize_mx(
+                    codes[name, a][:, first:last].bitcast(FP8X4), planes[name, a][:, first:last], grouped[:]
+                )
+
+        def moving(name, a):
+            if name in packed_words:
+                return (
+                    packed_words[name][:, a * 2 * N : (a + 1) * 2 * N].bitcast(FP4X4),
+                    packed_scales[name][:, a * N : (a + 1) * N],
+                )
+            return codes[name, a][:].bitcast(FP8X4), planes[name, a][:]
+
+        def stationary(name, a, b):
+            h, first = divmod(b * BLOCK, HALF)
+            plane = picked_scales[name, h] if a == 0 else moved_scales[name, h]
+            return parted[name, a, b].bitcast(FP4X4), plane[:, first : first + BLOCK]
+
+        def product(bank, terms, b):
+            steps = [(w, v, a) for w, v in terms for a in range(PASSES)]
+            for s, (w, v, a) in enumerate(steps):
+                lhs, lhs_scale = stationary(v, a, b)
+                rhs, rhs_scale = moving(w, a)
+                nc.tensor.matmul_mx(
+                    bank[:], lhsT=lhs, lhsT_scale=lhs_scale, rhs=rhs, rhs_scale=rhs_scale,
+                    start=(s == 0), stop=(s == len(steps) - 1),
+                )
+
+        def dealt(bank):
+            return bank[:].rearrange("p (m t) -> p t m", t=PACK)
+
+        messages, gate_sums, source_sums = {}, {}, {}
+
+        def bank(letter, name):
+            return psum.tile([P, N], F32, name=name, tag="bank" + letter)
+
+        def gate_products(b, banks):
+            gate_sums[b] = bank(banks[0], "za%d" % b)
+            product(gate_sums[b], [("wa", "dst"), ("wb", "src")], b)
+            source_sums[b] = bank(banks[1], "ms%d" % b)
+            product(source_sums[b], [("wc", "src")], b)
+
+        def gate(b):
+            eta = held([P, PACK, P], F32, "eta%d" % b, ("wo_raw1_0", "wo_raw0_0")[b % 2])
+            nc.scalar.activation(eta[:], dealt(gate_sums[b]), ACT.Sigmoid)
+            messages[b] = held([P, PACK, P], F32, "message%d" % b)
+            nc.vector.tensor_tensor(messages[b][:], dealt(source_sums[b]), eta[:], MULT)
+
+        result = held([P, PACK, J], F32, "result")
+
+        def finish(blocks, own_banks, turn_banks):
+            own = {}
+            for b, letter in zip(blocks, own_banks):
+                ow = bank(letter, "ow%d" % b)
+                product(ow, [("wo", "dst")], b)
+                own[b] = ring.tile([P, PACK, P], F32, name="own")
+                nc.scalar.copy(own[b][:], dealt(ow))
+            for b, letter in zip(blocks, turn_banks):
+                turned = bank(letter, "turned%d" % b)
+                for t in range(PACK):
+                    cols = slice(t * BLOCK, (t + 1) * BLOCK)
+                    nc.tensor.matmul(turned[:, cols], messages[b][:, t, :], identity[:], start=True, stop=False, is_transpose=True)
+                    nc.tensor.matmul(turned[:, cols], own[b][:, t, :], identity[:], start=False, stop=True, is_transpose=True)
+                nc.scalar.activation(
+                    result[:, :, b * BLOCK : (b + 1) * BLOCK], turned[:].rearrange("p (t j) -> p t j", t=PACK), ACT.Relu
+                )
+
+        def scatter(t, first, last):
+            nc.vector.tensor_tensor(
+                pages[t][:].indirect(dst_list[:, first // 16 : last // 16]),
+                result[:, t, first:last], edge_weight[:, first:last], MULT,
+            )
+
+        pairs = [held([P, 2, CHUNK, 2], BF16, "pairs%d" % c) for c in range(CHUNKS)]
+        out_rows = out_0.rearrange("(p t) c -> t p c", t=PACK)
+
+        def round_page(t, c, copy):
+            copy(pairs[c][:, t // 2, :, t % 2], pages[t][:, c * CHUNK : (c + 1) * CHUNK])
+
+        def page_done(t):
+            nc.sync.dma_start(out_rows[t], pages[t][:])
+            for c in range(CHUNKS):
+                round_page(t, c, nc.scalar.copy)
+
+        pick_scales(0)
+        pick_words(0, 256, {})
+        pick_words(256, 512, {})
+        for a in range(PASSES):
+            quantize_weight("wb", a, [(0, N, nc.scalar.copy)])
+        quantize_weight("wo", 0, [(0, N, nc.scalar.copy)])
+        quantize_weight("wo", 1, [(0, N // 2, nc.scalar.copy), (N // 2, N, nc.vector.tensor_copy)])
+        pick_scales(1)
+        edge_weight = held([P, J], F32, "edge_weight", "table_scales")
+        nc.sync.dma_start(edge_weight[:], wgo)
+        for b, banks in enumerate(("AC", "BD", "EG", "FH")):
+            gate_products(b, banks)
+        for b in (0, 1):
+            gate(b)
+        finish((0, 1), "AB", "CD")
+        for b in (2, 3):
+            gate(b)
+        pick_words(512, J, {"src": "wo_grouped0_0", "dst": "wo_grouped1_0"})
+        for t in range(PACK):
+            scatter(t, 0, 256)
+        for b, banks in ((4, "AB"), (5, "CD")):
+            gate_products(b, banks)
+            gate(b)
+        finish((2, 3), "EF", "GH")
+        for t in range(3):
+            scatter(t, 256, 512)
+        for b, banks in ((6, "AE"), (7, "CF")):
+            gate_products(b, banks)
+            gate(b)
+        finish((4, 5), "GH", "AC")
+        for t in (0, 1):
+            scatter(t, 512, 768)
+        finish((6, 7), "GH", "BD")
+        for t in (0, 1):
+            scatter(t, 768, J)
+            page_done(t)
+        scatter(2, 512, J)
+        page_done(2)
+        scatter(3, 256, J)
+        nc.sync.dma_start(out_rows[3], pages[3][:])
+
+        out_codes = held([P, T], U32, "out_codes")
+        out_plane = held([P, T], U8, "out_plane")
+        code_rows = out_1[0].rearrange("p t b -> p (t b)").bitcast(I32)
+        woven = [held([P, CHUNK * PACK], BF16, "woven%d" % c) for c in range(CHUNKS)]
+
+        def weave(c, copy):
+            copy(
+                woven[c][:].bitcast(F32).rearrange("p (c u) -> p c u", u=2),
+                pairs[c][:].rearrange("p u c e -> p u (c e)").bitcast(F32).rearrange("p u c -> p c u"),
+            )
+
+        def quantize_out(c):
+            cols = slice(c * CHUNK, (c + 1) * CHUNK)
+            nc.vector.quantize_mx(out_codes[:, cols].bitcast(FP8X4), out_plane[:, cols], woven[c][:])
+            if c % 2 == 1:
+                cols = slice((c - 1) * CHUNK, (c + 1) * CHUNK)
+                nc.sync.dma_start(code_rows[:, cols], out_codes[:, cols].bitcast(I32))
+
+        for c in range(CHUNKS):
+            round_page(3, c, nc.scalar.copy)
+        for c in range(CHUNKS - 2, CHUNKS):
+            weave(c, nc.scalar.copy)
+        weave(0, nc.vector.tensor_copy)
+        for c in range(CHUNKS):
+            if c + 1 < CHUNKS - 2:
+                weave(c + 1, nc.vector.tensor_copy)
+            quantize_out(c)
+        plane_rows = out_2[0].bitcast(I32)
+        for q in range(4):
+            queue = nc.sync if q % 2 == 0 else nc.scalar
+            queue.dma_start(plane_rows[4 * q : 4 * q + 4, :], out_plane[32 * q : 32 * q + 4, :].bitcast(I32))

@@ -47,11 +47,6 @@ def tile_list_rgg_ownreluP_kernel(
 
         table_scales = held([P, T], U8, "table_scales")
         nc.gpsimd.memset(table_scales[:].bitcast(I32), 0)
-        table_words = held([P, T], I32, "table_words")
-        nc.sync.dma_start(table_words[:], tab_words[0].rearrange("p t b -> p (t b)").bitcast(I32))
-        scale_rows = tab_scales.rearrange("a (q r) t -> r q a t", r=4)
-        for r in range(4):
-            nc.sync.dma_start(table_scales[r:P:16, :].bitcast(I32), scale_rows[r].bitcast(I32))
 
         warm = held([P, 1], F32, "warm")
         nc.gpsimd.memset(warm[:], 0.0)
@@ -87,35 +82,38 @@ def tile_list_rgg_ownreluP_kernel(
 
         raw = {}
 
-        def load_raw(name, w, a, first, last):
-            raw[name, a, first] = held([P, PACK, last - first], F32, "%s_raw%d_%d" % (name, a, first))
+        def load_raw(name, w, a, first, last, tag=""):
+            raw[name, a, first] = held([P, PACK, last - first], F32, "%s_raw%d_%d" % (name, a, first), tag)
             rows = w[a * P * PACK : (a + 1) * P * PACK, first:last]
             nc.sync.dma_start(raw[name, a, first][:], rows.rearrange("(p i) n -> p i n", i=PACK))
 
         load_raw("wb", wb, 0, 0, N)
-        load_raw("wb", wb, 1, 0, N)
+        scale_rows = tab_scales.rearrange("a (q r) t -> r q a t", r=4)
+        for r in range(4):
+            nc.sync.dma_start(table_scales[r:P:16, :].bitcast(I32), scale_rows[r].bitcast(I32))
         load_packed_words("wa", wa_words)
+        table_words = held([P, T], I32, "table_words")
+        nc.sync.dma_start(table_words[:], tab_words[0].rearrange("p t b -> p (t b)").bitcast(I32))
         load_packed_scales("wa", wa_scales)
+        load_raw("wb", wb, 1, 0, N)
         load_packed_words("wc", wc_words)
-        load_raw("wo", wo, 0, 0, N)
         load_packed_scales("wc", wc_scales)
+        load_raw("wo", wo, 0, 0, N)
         load_raw("wo", wo, 1, 0, N // 2)
         load_raw("wo", wo, 1, N // 2, N)
 
         pages = [held([P, T], F32, "page%d" % t) for t in range(PACK)]
-        for t in range(PACK):
-            engine = nc.vector if t < 2 else nc.gpsimd
-            engine.memset(pages[t][:].bitcast(I32), 0)
+        for t in range(4):
+            nc.vector.memset(pages[t][:].bitcast(I32), 0)
 
         picked_scales = {}
 
-        def pick_scales(h):
+        def pick_scales(h, after):
             cols = slice(h * HALF // 16, (h + 1) * HALF // 16)
             for name in ("dst", "src"):
-                after = {("dst", 1): "wb_grouped0_0", ("src", 1): "wb_grouped1_0"}.get((name, h), "")
-                picked_scales[name, h] = held([P, HALF], U8, "%s_picked_scales%d" % (name, h), after)
+                picked_scales[name, h] = held([P, HALF], U8, "%s_picked_scales%d" % (name, h), after.get(name, ""))
                 nc.vector.tensor_copy(picked_scales[name, h][:], table_scales[:].indirect(lists[name][:, cols]))
-                nc.gpsimd.dma_start(
+                nc.sync.dma_start(
                     moved_scales[name, h][0 : P - 16, :].bitcast(I32), picked_scales[name, h][16:P, :].bitcast(I32)
                 )
 
@@ -169,7 +167,7 @@ def tile_list_rgg_ownreluP_kernel(
             return parted[name, a, b].bitcast(FP4X4), plane[:, first : first + BLOCK]
 
         def product(bank, terms, b):
-            steps = [(w, v, a) for w, v in terms for a in range(PASSES)]
+            steps = [(w, v, a) for a in range(PASSES) for w, v in terms]
             for s, (w, v, a) in enumerate(steps):
                 lhs, lhs_scale = stationary(v, a, b)
                 rhs, rhs_scale = moving(w, a)
@@ -193,20 +191,25 @@ def tile_list_rgg_ownreluP_kernel(
             product(source_sums[b], [("wc", "src")], b)
 
         def gate(b):
-            eta = held([P, PACK, P], F32, "eta%d" % b, ("wo_raw1_0", "wo_raw0_0")[b % 2])
+            eta = held([P, PACK, P], F32, "eta%d" % b, ("wo_raw0_0", "wo_raw1_0", "eta2", "eta3")[b % 4])
             nc.scalar.activation(eta[:], dealt(gate_sums[b]), ACT.Sigmoid)
             messages[b] = held([P, PACK, P], F32, "message%d" % b)
             nc.vector.tensor_tensor(messages[b][:], dealt(source_sums[b]), eta[:], MULT)
 
         result = held([P, PACK, J], F32, "result")
 
-        def finish(blocks, own_banks, turn_banks):
+        own_sums = {}
+
+        def own_products(blocks, banks):
+            for b, letter in zip(blocks, banks):
+                own_sums[b] = bank(letter, "ow%d" % b)
+                product(own_sums[b], [("wo", "dst")], b)
+
+        def finish(blocks, turn_banks):
             own = {}
-            for b, letter in zip(blocks, own_banks):
-                ow = bank(letter, "ow%d" % b)
-                product(ow, [("wo", "dst")], b)
+            for b in blocks:
                 own[b] = ring.tile([P, PACK, P], F32, name="own")
-                nc.scalar.copy(own[b][:], dealt(ow))
+                nc.scalar.copy(own[b][:], dealt(own_sums[b]))
             for b, letter in zip(blocks, turn_banks):
                 turned = bank(letter, "turned%d" % b)
                 for t in range(PACK):
@@ -234,43 +237,48 @@ def tile_list_rgg_ownreluP_kernel(
             for c in range(CHUNKS):
                 round_page(t, c, nc.scalar.copy)
 
-        pick_scales(0)
+        pick_scales(0, {})
         pick_words(0, 256, {})
+        quantize_weight("wb", 0, [(0, N, nc.scalar.copy)])
         pick_words(256, 512, {})
-        for a in range(PASSES):
-            quantize_weight("wb", a, [(0, N, nc.scalar.copy)])
+        quantize_weight("wb", 1, [(0, N, nc.scalar.copy)])
+        pick_scales(1, {"dst": "wb_grouped1_0", "src": "wb_raw1_0"})
+        pick_words(512, 768, {"dst": "dst_picked0", "src": "src_picked0"})
         quantize_weight("wo", 0, [(0, N, nc.scalar.copy)])
         quantize_weight("wo", 1, [(0, N // 2, nc.scalar.copy), (N // 2, N, nc.vector.tensor_copy)])
-        pick_scales(1)
         edge_weight = held([P, J], F32, "edge_weight", "table_scales")
         nc.sync.dma_start(edge_weight[:], wgo)
         for b, banks in enumerate(("AC", "BD", "EG", "FH")):
             gate_products(b, banks)
-        for b in (0, 1):
+        for b in range(4):
             gate(b)
-        finish((0, 1), "AB", "CD")
-        for b in (2, 3):
+        own_products((0, 1), "AB")
+        for b, banks in ((4, "EC"), (5, "FD")):
+            gate_products(b, banks)
             gate(b)
-        pick_words(512, J, {"src": "wo_grouped0_0", "dst": "wo_grouped1_0"})
+        finish((0, 1), "AB")
+        pick_words(768, J, {"src": "wo_grouped1_256", "dst": "wo_grouped1_0"})
+        for t in range(4, PACK):
+            nc.vector.memset(pages[t][:].bitcast(I32), 0)
         for t in range(PACK):
             scatter(t, 0, 256)
-        for b, banks in ((4, "AB"), (5, "CD")):
+        for b, banks in ((6, "EG"), (7, "FH")):
             gate_products(b, banks)
             gate(b)
-        finish((2, 3), "EF", "GH")
-        for t in range(3):
+        own_products((2, 3), "CD")
+        finish((2, 3), "AB")
+        for t in range(2):
             scatter(t, 256, 512)
-        for b, banks in ((6, "AE"), (7, "CF")):
-            gate_products(b, banks)
-            gate(b)
-        finish((4, 5), "GH", "AC")
+        own_products((4, 5), "EF")
+        finish((4, 5), "CD")
         for t in (0, 1):
             scatter(t, 512, 768)
-        finish((6, 7), "GH", "BD")
+        own_products((6, 7), "AB")
+        finish((6, 7), "GH")
         for t in (0, 1):
             scatter(t, 768, J)
             page_done(t)
-        scatter(2, 512, J)
+        scatter(2, 256, J)
         page_done(2)
         scatter(3, 256, J)
         nc.sync.dma_start(out_rows[3], pages[3][:])

@@ -59,12 +59,6 @@ def tile_list_rgg_ownreluP_kernel(
             packed_scales[name] = held([P, PASSES * N], U8, name + "_scales")
             nc.gpsimd.memset(packed_scales[name][:].bitcast(I32), 0)
         moved_scales = {}
-        for h in range(2):
-            for name in ("dst", "src"):
-                moved_scales[name, h] = held([P, HALF], U8, "%s_moved_scales%d" % (name, h))
-                nc.gpsimd.memset(moved_scales[name, h][:].bitcast(I32), 0)
-        identity = held([P, P], F32, "identity")
-        make_identity(nc, identity[:])
 
         def load_packed_words(name, words):
             nc.sync.dma_start(
@@ -140,17 +134,21 @@ def tile_list_rgg_ownreluP_kernel(
 
         codes, planes = {}, {}
 
-        def quantize_weight(name, a, parts):
-            codes[name, a] = held([P, N], U32, "%s_codes%d" % (name, a))
+        grouped = {}
+
+        def round_weight(name, a, first, last, copy, slot=""):
+            grouped[name, a, first] = held([P, (last - first) * PACK], BF16, "%s_grouped%d_%d" % (name, a, first), slot)
+            copy(
+                grouped[name, a, first][:].rearrange("p (c m i) -> p c i m", m=4, i=PACK),
+                raw[name, a, first][:].rearrange("p i (c m) -> p c i m", m=4),
+            )
+
+        def quantize_weight(name, a, parts, slot=""):
+            codes[name, a] = held([P, N], U32, "%s_codes%d" % (name, a), slot)
             planes[name, a] = held([P, N], U8, "%s_plane%d" % (name, a))
-            for first, last, copy in parts:
-                grouped = held([P, (last - first) * PACK], BF16, "%s_grouped%d_%d" % (name, a, first))
-                copy(
-                    grouped[:].rearrange("p (c m i) -> p c i m", m=4, i=PACK),
-                    raw[name, a, first][:].rearrange("p i (c m) -> p c i m", m=4),
-                )
+            for first, last in parts:
                 nc.vector.quantize_mx(
-                    codes[name, a][:, first:last].bitcast(FP8X4), planes[name, a][:, first:last], grouped[:]
+                    codes[name, a][:, first:last].bitcast(FP8X4), planes[name, a][:, first:last], grouped[name, a, first][:]
                 )
 
         def moving(name, a):
@@ -191,7 +189,7 @@ def tile_list_rgg_ownreluP_kernel(
             product(source_sums[b], [("wc", "src")], b)
 
         def gate(b):
-            eta = held([P, PACK, P], F32, "eta%d" % b, ("wo_raw0_0", "wo_raw1_0", "eta2", "eta3")[b % 4])
+            eta = held([P, PACK, P], F32, "eta%d" % b, ("wo_raw0_0", "wo_raw1_0", "eta2", "eta3", "eta4", "eta5", "eta2", "eta3")[b])
             nc.scalar.activation(eta[:], dealt(gate_sums[b]), ACT.Sigmoid)
             messages[b] = held([P, PACK, P], F32, "message%d" % b)
             nc.vector.tensor_tensor(messages[b][:], dealt(source_sums[b]), eta[:], MULT)
@@ -235,29 +233,40 @@ def tile_list_rgg_ownreluP_kernel(
         def page_done(t):
             nc.sync.dma_start(out_rows[t], pages[t][:])
             for c in range(CHUNKS):
-                round_page(t, c, nc.scalar.copy)
+                round_page(t, c, nc.vector.tensor_copy if t >= 2 and c < 2 else nc.scalar.copy)
 
+        round_weight("wb", 0, 0, N, nc.scalar.copy)
+        moved_planes = held([P, 2 * J], U8, "moved_planes", "wb_raw0_0")
+        nc.gpsimd.memset(moved_planes[:].bitcast(I32), 0)
+        for i, key in enumerate((name, h) for h in range(2) for name in ("dst", "src")):
+            moved_scales[key] = moved_planes[:, i * HALF : (i + 1) * HALF]
         pick_scales(0, {})
         pick_words(0, 256, {})
-        quantize_weight("wb", 0, [(0, N, nc.scalar.copy)])
+        quantize_weight("wb", 0, [(0, N)])
         pick_words(256, 512, {})
-        quantize_weight("wb", 1, [(0, N, nc.scalar.copy)])
+        round_weight("wb", 1, 0, N, nc.scalar.copy)
+        quantize_weight("wb", 1, [(0, N)])
         pick_scales(1, {"dst": "wb_grouped1_0", "src": "wb_raw1_0"})
         pick_words(512, 768, {"dst": "dst_picked0", "src": "src_picked0"})
-        quantize_weight("wo", 0, [(0, N, nc.scalar.copy)])
-        quantize_weight("wo", 1, [(0, N // 2, nc.scalar.copy), (N // 2, N, nc.vector.tensor_copy)])
+        round_weight("wo", 0, 0, N, nc.scalar.copy)
+        round_weight("wo", 1, 0, N // 2, nc.scalar.copy)
         edge_weight = held([P, J], F32, "edge_weight", "table_scales")
         nc.sync.dma_start(edge_weight[:], wgo)
+        identity = held([P, P], F32, "identity", "wb_grouped0_0")
+        make_identity(nc, identity[:])
         for b, banks in enumerate(("AC", "BD", "EG", "FH")):
             gate_products(b, banks)
         for b in range(4):
             gate(b)
+        round_weight("wo", 1, N // 2, N, nc.vector.tensor_copy, "")
+        quantize_weight("wo", 0, [(0, N)], "")
+        quantize_weight("wo", 1, [(0, N // 2), (N // 2, N)], "")
         own_products((0, 1), "AB")
         for b, banks in ((4, "EC"), (5, "FD")):
             gate_products(b, banks)
             gate(b)
         finish((0, 1), "AB")
-        pick_words(768, J, {"src": "wo_grouped1_256", "dst": "wo_grouped1_0"})
+        pick_words(768, J, {"src": "eta2", "dst": "eta3"})
         for t in range(4, PACK):
             nc.vector.memset(pages[t][:].bitcast(I32), 0)
         for t in range(PACK):
@@ -267,7 +276,7 @@ def tile_list_rgg_ownreluP_kernel(
             gate(b)
         own_products((2, 3), "CD")
         finish((2, 3), "AB")
-        for t in range(2):
+        for t in range(3):
             scatter(t, 256, 512)
         own_products((4, 5), "EF")
         finish((4, 5), "CD")
@@ -278,7 +287,7 @@ def tile_list_rgg_ownreluP_kernel(
         for t in (0, 1):
             scatter(t, 768, J)
             page_done(t)
-        scatter(2, 256, J)
+        scatter(2, 512, J)
         page_done(2)
         scatter(3, 256, J)
         nc.sync.dma_start(out_rows[3], pages[3][:])
@@ -302,12 +311,12 @@ def tile_list_rgg_ownreluP_kernel(
                 nc.sync.dma_start(code_rows[:, cols], out_codes[:, cols].bitcast(I32))
 
         for c in range(CHUNKS):
-            round_page(3, c, nc.scalar.copy)
-        for c in range(CHUNKS - 2, CHUNKS):
+            round_page(3, c, nc.vector.tensor_copy if c < 2 else nc.scalar.copy)
+        for c in range(CHUNKS - 3, CHUNKS):
             weave(c, nc.scalar.copy)
         weave(0, nc.vector.tensor_copy)
         for c in range(CHUNKS):
-            if c + 1 < CHUNKS - 2:
+            if c + 1 < CHUNKS - 3:
                 weave(c + 1, nc.vector.tensor_copy)
             quantize_out(c)
         plane_rows = out_2[0].bitcast(I32)

@@ -81,16 +81,16 @@ def tile_list_rgg_ownreluP_kernel(
             rows = w[a * P * PACK : (a + 1) * P * PACK, first:last]
             nc.sync.dma_start(raw[name, a, first][:], rows.rearrange("(p i) n -> p i n", i=PACK))
 
-        load_raw("wb", wb, 0, 0, N)
         scale_rows = tab_scales.rearrange("a (q r) t -> r q a t", r=4)
         for r in range(4):
             nc.sync.dma_start(table_scales[r:P:16, :].bitcast(I32), scale_rows[r].bitcast(I32))
-        load_packed_words("wa", wa_words)
         table_words = held([P, T], I32, "table_words")
         nc.sync.dma_start(table_words[:], tab_words[0].rearrange("p t b -> p (t b)").bitcast(I32))
+        load_packed_words("wa", wa_words)
+        load_packed_words("wc", wc_words)
+        load_raw("wb", wb, 0, 0, N)
         load_packed_scales("wa", wa_scales)
         load_raw("wb", wb, 1, 0, N)
-        load_packed_words("wc", wc_words)
         load_packed_scales("wc", wc_scales)
         load_raw("wo", wo, 0, 0, N)
         load_raw("wo", wo, 1, 0, N // 2)
@@ -98,7 +98,7 @@ def tile_list_rgg_ownreluP_kernel(
 
         pages = [held([P, T], F32, "page%d" % t) for t in range(PACK)]
         for t in range(4):
-            nc.vector.memset(pages[t][:].bitcast(I32), 0)
+            (nc.vector if t < 2 else nc.gpsimd).memset(pages[t][:].bitcast(I32), 0)
 
         picked_scales = {}
 
@@ -212,8 +212,8 @@ def tile_list_rgg_ownreluP_kernel(
                 turned = bank(letter, "turned%d" % b)
                 for t in range(PACK):
                     cols = slice(t * BLOCK, (t + 1) * BLOCK)
-                    nc.tensor.matmul(turned[:, cols], messages[b][:, t, :], identity[:], start=True, stop=False, is_transpose=True)
-                    nc.tensor.matmul(turned[:, cols], own[b][:, t, :], identity[:], start=False, stop=True, is_transpose=True)
+                    nc.tensor.matmul(turned[:, cols], own[b][:, t, :], identity[:], start=True, stop=False, is_transpose=True)
+                    nc.tensor.matmul(turned[:, cols], messages[b][:, t, :], identity[:], start=False, stop=True, is_transpose=True)
                 nc.scalar.activation(
                     result[:, :, b * BLOCK : (b + 1) * BLOCK], turned[:].rearrange("p (t j) -> p t j", t=PACK), ACT.Relu
                 )
@@ -246,8 +246,7 @@ def tile_list_rgg_ownreluP_kernel(
         pick_words(256, 512, {})
         round_weight("wb", 1, 0, N, nc.scalar.copy)
         quantize_weight("wb", 1, [(0, N)])
-        pick_scales(1, {"dst": "wb_grouped1_0", "src": "wb_raw1_0"})
-        pick_words(512, 768, {"dst": "dst_picked0", "src": "src_picked0"})
+        pick_scales(1, {"dst": "dst_picked256", "src": "src_picked256"})
         round_weight("wo", 0, 0, N, nc.scalar.copy)
         round_weight("wo", 1, 0, N // 2, nc.scalar.copy)
         edge_weight = held([P, J], F32, "edge_weight", "table_scales")
@@ -261,29 +260,29 @@ def tile_list_rgg_ownreluP_kernel(
         round_weight("wo", 1, N // 2, N, nc.vector.tensor_copy, "")
         quantize_weight("wo", 0, [(0, N)], "")
         quantize_weight("wo", 1, [(0, N // 2), (N // 2, N)], "")
+        pick_words(512, 768, {"dst": "wb_grouped1_0", "src": "wb_raw1_0"})
         own_products((0, 1), "AB")
-        for b, banks in ((4, "EC"), (5, "FD")):
-            gate_products(b, banks)
-            gate(b)
+        gate_products(4, "EC")
+        gate(4)
         finish((0, 1), "AB")
         pick_words(768, J, {"src": "eta2", "dst": "eta3"})
-        for t in range(4, PACK):
-            nc.vector.memset(pages[t][:].bitcast(I32), 0)
         for t in range(PACK):
             scatter(t, 0, 256)
-        for b, banks in ((6, "EG"), (7, "FH")):
+        for b, banks in ((5, "FD"), (6, "EG")):
             gate_products(b, banks)
             gate(b)
-        own_products((2, 3), "CD")
+        own_products((2, 3), "HC")
         finish((2, 3), "AB")
         for t in range(3):
             scatter(t, 256, 512)
-        own_products((4, 5), "EF")
-        finish((4, 5), "CD")
+        gate_products(7, "FH")
+        gate(7)
+        own_products((4, 5), "CA")
+        finish((4, 5), "BF")
         for t in (0, 1):
             scatter(t, 512, 768)
-        own_products((6, 7), "AB")
-        finish((6, 7), "GH")
+        own_products((6, 7), "CA")
+        finish((6, 7), "DG")
         for t in (0, 1):
             scatter(t, 768, J)
             page_done(t)

@@ -20,11 +20,18 @@ MULT = mybir.AluOpType.mult
 P = 128
 PACK = 4
 PASSES = K // (P * PACK)
+LIST_ROWS = 16
+QUADRANT = 32
+PLANE_ROWS = 4
+SECOND_PASS_ROW = 16
+LINE = 4
 BLOCK = 128
-BLOCKS = J // BLOCK
+QUARTER = J // 4
 HALF = J // 2
 CHUNK = 256
 CHUNKS = T // CHUNK
+VECTOR_ROUNDS = 2
+SCALAR_WEAVES = 3
 
 
 def tile_list_rgg_ownreluP_kernel(
@@ -36,29 +43,33 @@ def tile_list_rgg_ownreluP_kernel(
         ring = ctx.enter_context(tc.tile_pool(name="ring", bufs=2))
         psum = ctx.enter_context(tc.psum_pool(name="psum", bufs=1))
 
-        def held(shape, dtype, name, tag=""):
-            return keep.tile(shape, dtype, name=name, tag=tag or name, align_bytes=64)
+        def held(shape, dtype, name, slot=""):
+            return keep.tile(shape, dtype, name=name, tag=slot or name, align_bytes=64)
 
-        src_list = keep.tile([P, J // 16], U16, name="src_list")
-        dst_list = keep.tile([P, J // 16], U16, name="dst_list")
+        src_list = keep.tile([P, J // LIST_ROWS], U16, name="src_list")
+        dst_list = keep.tile([P, J // LIST_ROWS], U16, name="dst_list")
         nc.sync.dma_start(src_list[:], offs)
         nc.sync.dma_start(dst_list[:], offs2)
         lists = {"src": src_list, "dst": dst_list}
 
+        def entries(name, first, last):
+            return lists[name][:, first // LIST_ROWS : last // LIST_ROWS]
+
         table_scales = held([P, T], U8, "table_scales")
         nc.gpsimd.memset(table_scales[:].bitcast(I32), 0)
-
-        warm = held([P, 1], F32, "warm")
-        nc.gpsimd.memset(warm[:], 0.0)
-        warm_out = held([P, 1], F32, "warm_out")
-        nc.scalar.activation(warm_out[:], warm[:], ACT.Sigmoid)
-
+        weight_planes = held([P, 2 * PASSES * N], U8, "weight_planes")
+        nc.vector.memset(weight_planes[:].bitcast(I32), 0)
         packed_words, packed_scales = {}, {}
-        for name in ("wa", "wc"):
+        for i, name in enumerate(("wa", "wc")):
             packed_words[name] = held([P, PASSES * 2 * N], U8, name + "_words")
-            packed_scales[name] = held([P, PASSES * N], U8, name + "_scales")
-            nc.gpsimd.memset(packed_scales[name][:].bitcast(I32), 0)
+            packed_scales[name] = weight_planes[:, i * PASSES * N : (i + 1) * PASSES * N]
+        moved_planes = held([P, 2 * J], U8, "moved_planes")
+        nc.vector.memset(moved_planes[:].bitcast(I32), 0)
         moved_scales = {}
+        for i, key in enumerate((name, h) for h in range(2) for name in ("dst", "src")):
+            moved_scales[key] = moved_planes[:, i * HALF : (i + 1) * HALF]
+        identity = held([P, P], F32, "identity")
+        make_identity(nc, identity[:])
 
         def load_packed_words(name, words):
             nc.sync.dma_start(
@@ -67,89 +78,79 @@ def tile_list_rgg_ownreluP_kernel(
             )
 
         def load_packed_scales(name, scales):
-            rows = scales.rearrange("a (q r) n -> r q a n", r=4)
-            for r in range(4):
+            rows = scales.rearrange("a (q r) n -> r q a n", r=PLANE_ROWS)
+            for r in range(PLANE_ROWS):
                 nc.sync.dma_start(
-                    packed_scales[name][r:P:32, :].bitcast(I32).rearrange("q (a c) -> q a c", a=PASSES),
+                    packed_scales[name][r:P:QUADRANT, :].bitcast(I32).rearrange("q (a c) -> q a c", a=PASSES),
                     rows[r].bitcast(I32),
                 )
 
         raw = {}
 
-        def load_raw(name, w, a, first, last, tag=""):
-            raw[name, a, first] = held([P, PACK, last - first], F32, "%s_raw%d_%d" % (name, a, first), tag)
-            rows = w[a * P * PACK : (a + 1) * P * PACK, first:last]
-            nc.sync.dma_start(raw[name, a, first][:], rows.rearrange("(p i) n -> p i n", i=PACK))
+        def load_raw(name, w, a):
+            raw[name, a] = held([P, PACK, N], F32, "%s_raw%d" % (name, a))
+            rows = w[a * P * PACK : (a + 1) * P * PACK, :]
+            nc.sync.dma_start(raw[name, a][:], rows.rearrange("(p i) n -> p i n", i=PACK))
 
-        scale_rows = tab_scales.rearrange("a (q r) t -> r q a t", r=4)
-        for r in range(4):
-            nc.sync.dma_start(table_scales[r:P:16, :].bitcast(I32), scale_rows[r].bitcast(I32))
-        table_words = held([P, T], I32, "table_words")
-        nc.sync.dma_start(table_words[:], tab_words[0].rearrange("p t b -> p (t b)").bitcast(I32))
+        scale_rows = tab_scales.rearrange("a (q r) t -> r q a t", r=PLANE_ROWS)
+        for r in range(PLANE_ROWS):
+            nc.sync.dma_start(table_scales[r:P:SECOND_PASS_ROW, :].bitcast(I32), scale_rows[r].bitcast(I32))
+        load_raw("wb", wb, 0)
         load_packed_words("wa", wa_words)
         load_packed_words("wc", wc_words)
-        load_raw("wb", wb, 0, 0, N)
+        table_words = held([P, T], I32, "table_words")
+        nc.sync.dma_start(table_words[:], tab_words[0].rearrange("p t b -> p (t b)").bitcast(I32))
         load_packed_scales("wa", wa_scales)
-        load_raw("wb", wb, 1, 0, N)
+        load_raw("wb", wb, 1)
         load_packed_scales("wc", wc_scales)
-        load_raw("wo", wo, 0, 0, N)
-        load_raw("wo", wo, 1, 0, N // 2)
-        load_raw("wo", wo, 1, N // 2, N)
+        load_raw("wo", wo, 0)
+        load_raw("wo", wo, 1)
 
         pages = [held([P, T], F32, "page%d" % t) for t in range(PACK)]
-        for t in range(4):
-            (nc.vector if t < 2 else nc.gpsimd).memset(pages[t][:].bitcast(I32), 0)
+        for t in range(PACK):
+            nc.vector.memset(pages[t][:].bitcast(I32), 0)
 
-        picked_scales = {}
+        picked_scales, parted = {}, {}
 
-        def pick_scales(h, after):
-            cols = slice(h * HALF // 16, (h + 1) * HALF // 16)
+        def pick_scales(h, slots):
             for name in ("dst", "src"):
-                picked_scales[name, h] = held([P, HALF], U8, "%s_picked_scales%d" % (name, h), after.get(name, ""))
-                nc.vector.tensor_copy(picked_scales[name, h][:], table_scales[:].indirect(lists[name][:, cols]))
+                picked_scales[name, h] = held([P, HALF], U8, "%s_picked_scales%d" % (name, h), slots.get(name, ""))
+                nc.vector.tensor_copy(
+                    picked_scales[name, h][:], table_scales[:].indirect(entries(name, h * HALF, (h + 1) * HALF))
+                )
                 nc.sync.dma_start(
-                    moved_scales[name, h][0 : P - 16, :].bitcast(I32), picked_scales[name, h][16:P, :].bitcast(I32)
+                    moved_scales[name, h][0 : P - SECOND_PASS_ROW, :].bitcast(I32),
+                    picked_scales[name, h][SECOND_PASS_ROW:P, :].bitcast(I32),
                 )
 
-        parted = {}
-
-        def pick_words(first, last, after):
+        def pick_words(q, slots):
             picked = {}
-            width = last - first
             for name in ("dst", "src"):
-                picked[name] = held([P, width], U32, "%s_picked%d" % (name, first), after.get(name, ""))
+                picked[name] = held([P, QUARTER], U32, "%s_picked%d" % (name, q), slots.get(name, ""))
                 nc.vector.tensor_copy(
-                    picked[name][:], table_words[:].bitcast(U32).indirect(lists[name][:, first // 16 : last // 16])
+                    picked[name][:], table_words[:].bitcast(U32).indirect(entries(name, q * QUARTER, (q + 1) * QUARTER))
                 )
             for name in ("dst", "src"):
-                words = held([P, PASSES * 2 * width], U8, "%s_parted%d" % (name, first))
+                parted[name, q] = held([P, PASSES * 2 * QUARTER], U8, "%s_parted%d" % (name, q))
                 nc.vector.tensor_copy(
-                    words[:].bitcast(U16).rearrange("p (a j) -> p a j", a=PASSES),
+                    parted[name, q][:].bitcast(U16).rearrange("p (a j) -> p a j", a=PASSES),
                     picked[name][:].bitcast(U16).rearrange("p (j a) -> p a j", a=PASSES),
                 )
-                for b in range(first // BLOCK, last // BLOCK):
-                    at = b * BLOCK - first
-                    for a in range(PASSES):
-                        parted[name, a, b] = words[:, 2 * (a * width + at) : 2 * (a * width + at + BLOCK)]
 
-        codes, planes = {}, {}
+        grouped, codes, planes = {}, {}, {}
 
-        grouped = {}
-
-        def round_weight(name, a, first, last, copy, slot=""):
-            grouped[name, a, first] = held([P, (last - first) * PACK], BF16, "%s_grouped%d_%d" % (name, a, first), slot)
-            copy(
-                grouped[name, a, first][:].rearrange("p (c m i) -> p c i m", m=4, i=PACK),
-                raw[name, a, first][:].rearrange("p i (c m) -> p c i m", m=4),
-            )
-
-        def quantize_weight(name, a, parts, slot=""):
-            codes[name, a] = held([P, N], U32, "%s_codes%d" % (name, a), slot)
-            planes[name, a] = held([P, N], U8, "%s_plane%d" % (name, a))
-            for first, last in parts:
-                nc.vector.quantize_mx(
-                    codes[name, a][:, first:last].bitcast(FP8X4), planes[name, a][:, first:last], grouped[name, a, first][:]
+        def round_weight(name, a, shares):
+            grouped[name, a] = held([P, N * PACK], BF16, "%s_grouped%d" % (name, a))
+            for copy, first, last in shares:
+                copy(
+                    grouped[name, a][:, first * PACK : last * PACK].rearrange("p (c m i) -> p c i m", m=LINE, i=PACK),
+                    raw[name, a][:, :, first:last].rearrange("p i (c m) -> p c i m", m=LINE),
                 )
+
+        def quantize_weight(name, a):
+            codes[name, a] = held([P, N], U32, "%s_codes%d" % (name, a))
+            planes[name, a] = held([P, N], U8, "%s_plane%d" % (name, a))
+            nc.vector.quantize_mx(codes[name, a][:].bitcast(FP8X4), planes[name, a][:], grouped[name, a][:])
 
         def moving(name, a):
             if name in packed_words:
@@ -160,136 +161,133 @@ def tile_list_rgg_ownreluP_kernel(
             return codes[name, a][:].bitcast(FP8X4), planes[name, a][:]
 
         def stationary(name, a, b):
-            h, first = divmod(b * BLOCK, HALF)
+            q, in_quarter = divmod(b * BLOCK, QUARTER)
+            h, in_half = divmod(b * BLOCK, HALF)
+            at = 2 * (a * QUARTER + in_quarter)
             plane = picked_scales[name, h] if a == 0 else moved_scales[name, h]
-            return parted[name, a, b].bitcast(FP4X4), plane[:, first : first + BLOCK]
+            return parted[name, q][:, at : at + 2 * BLOCK].bitcast(FP4X4), plane[:, in_half : in_half + BLOCK]
 
-        def product(bank, terms, b):
+        sums, bank_tags = {}, {}
+
+        def bank(name, after=""):
+            bank_tags[name] = bank_tags[after] if after else name
+            sums[name] = psum.tile([P, N], F32, name=name, tag=bank_tags[name])
+            return sums[name]
+
+        def product(result_bank, terms, b):
             steps = [(w, v, a) for a in range(PASSES) for w, v in terms]
             for s, (w, v, a) in enumerate(steps):
                 lhs, lhs_scale = stationary(v, a, b)
                 rhs, rhs_scale = moving(w, a)
                 nc.tensor.matmul_mx(
-                    bank[:], lhsT=lhs, lhsT_scale=lhs_scale, rhs=rhs, rhs_scale=rhs_scale,
+                    result_bank[:], lhsT=lhs, lhsT_scale=lhs_scale, rhs=rhs, rhs_scale=rhs_scale,
                     start=(s == 0), stop=(s == len(steps) - 1),
                 )
 
-        def dealt(bank):
-            return bank[:].rearrange("p (m t) -> p t m", t=PACK)
+        def dealt(name):
+            return sums[name][:].rearrange("p (m t) -> p t m", t=PACK)
 
-        messages, gate_sums, source_sums = {}, {}, {}
+        def gate_products(b, za_after="", ms_after=""):
+            product(bank("za%d" % b, za_after), [("wa", "dst"), ("wb", "src")], b)
+            product(bank("ms%d" % b, ms_after), [("wc", "src")], b)
 
-        def bank(letter, name):
-            return psum.tile([P, N], F32, name=name, tag="bank" + letter)
+        messages = {}
 
-        def gate_products(b, banks):
-            gate_sums[b] = bank(banks[0], "za%d" % b)
-            product(gate_sums[b], [("wa", "dst"), ("wb", "src")], b)
-            source_sums[b] = bank(banks[1], "ms%d" % b)
-            product(source_sums[b], [("wc", "src")], b)
-
-        def gate(b):
-            eta = held([P, PACK, P], F32, "eta%d" % b, ("wo_raw0_0", "wo_raw1_0", "eta2", "eta3", "eta4", "eta5", "eta2", "eta3")[b])
-            nc.scalar.activation(eta[:], dealt(gate_sums[b]), ACT.Sigmoid)
+        def gate(b, slot=""):
+            eta = held([P, PACK, P], F32, "eta%d" % b, slot)
+            nc.scalar.activation(eta[:], dealt("za%d" % b), ACT.Sigmoid)
             messages[b] = held([P, PACK, P], F32, "message%d" % b)
-            nc.vector.tensor_tensor(messages[b][:], dealt(source_sums[b]), eta[:], MULT)
+            nc.vector.tensor_tensor(messages[b][:], dealt("ms%d" % b), eta[:], MULT)
+
+        def own_products(blocks, afters):
+            for b, after in zip(blocks, afters):
+                product(bank("ow%d" % b, after), [("wo", "dst")], b)
 
         result = held([P, PACK, J], F32, "result")
 
-        own_sums = {}
-
-        def own_products(blocks, banks):
-            for b, letter in zip(blocks, banks):
-                own_sums[b] = bank(letter, "ow%d" % b)
-                product(own_sums[b], [("wo", "dst")], b)
-
-        def finish(blocks, turn_banks):
+        def finish(blocks, afters):
             own = {}
             for b in blocks:
                 own[b] = ring.tile([P, PACK, P], F32, name="own")
-                nc.scalar.copy(own[b][:], dealt(own_sums[b]))
-            for b, letter in zip(blocks, turn_banks):
-                turned = bank(letter, "turned%d" % b)
+                nc.scalar.copy(own[b][:], dealt("ow%d" % b))
+            for b, after in zip(blocks, afters):
+                turned = bank("turned%d" % b, after)
                 for t in range(PACK):
                     cols = slice(t * BLOCK, (t + 1) * BLOCK)
-                    nc.tensor.matmul(turned[:, cols], own[b][:, t, :], identity[:], start=True, stop=False, is_transpose=True)
-                    nc.tensor.matmul(turned[:, cols], messages[b][:, t, :], identity[:], start=False, stop=True, is_transpose=True)
+                    nc.tensor.matmul(
+                        turned[:, cols], own[b][:, t, :], identity[:], start=True, stop=False, is_transpose=True
+                    )
+                    nc.tensor.matmul(
+                        turned[:, cols], messages[b][:, t, :], identity[:], start=False, stop=True, is_transpose=True
+                    )
                 nc.scalar.activation(
                     result[:, :, b * BLOCK : (b + 1) * BLOCK], turned[:].rearrange("p (t j) -> p t j", t=PACK), ACT.Relu
                 )
 
-        def scatter(t, first, last):
+        def scatter(t, first_quarter, last_quarter):
+            first, last = first_quarter * QUARTER, (last_quarter + 1) * QUARTER
             nc.vector.tensor_tensor(
-                pages[t][:].indirect(dst_list[:, first // 16 : last // 16]),
-                result[:, t, first:last], edge_weight[:, first:last], MULT,
+                pages[t][:].indirect(entries("dst", first, last)), result[:, t, first:last], edge_weight[:, first:last], MULT
             )
 
         pairs = [held([P, 2, CHUNK, 2], BF16, "pairs%d" % c) for c in range(CHUNKS)]
         out_rows = out_0.rearrange("(p t) c -> t p c", t=PACK)
 
-        def round_page(t, c, copy):
-            copy(pairs[c][:, t // 2, :, t % 2], pages[t][:, c * CHUNK : (c + 1) * CHUNK])
-
         def page_done(t):
             nc.sync.dma_start(out_rows[t], pages[t][:])
             for c in range(CHUNKS):
-                round_page(t, c, nc.vector.tensor_copy if t >= 2 and c < 2 else nc.scalar.copy)
+                copy = nc.vector.tensor_copy if t >= 2 and c < VECTOR_ROUNDS else nc.scalar.copy
+                copy(pairs[c][:, t // 2, :, t % 2], pages[t][:, c * CHUNK : (c + 1) * CHUNK])
 
-        round_weight("wb", 0, 0, N, nc.scalar.copy)
-        moved_planes = held([P, 2 * J], U8, "moved_planes", "wb_raw0_0")
-        nc.gpsimd.memset(moved_planes[:].bitcast(I32), 0)
-        for i, key in enumerate((name, h) for h in range(2) for name in ("dst", "src")):
-            moved_scales[key] = moved_planes[:, i * HALF : (i + 1) * HALF]
+        on_scalar = [(nc.scalar.copy, 0, N)]
+        round_weight("wb", 0, on_scalar)
         pick_scales(0, {})
-        pick_words(0, 256, {})
-        quantize_weight("wb", 0, [(0, N)])
-        pick_words(256, 512, {})
-        round_weight("wb", 1, 0, N, nc.scalar.copy)
-        quantize_weight("wb", 1, [(0, N)])
-        pick_scales(1, {"dst": "dst_picked256", "src": "src_picked256"})
-        round_weight("wo", 0, 0, N, nc.scalar.copy)
-        round_weight("wo", 1, 0, N // 2, nc.scalar.copy)
+        pick_words(0, {})
+        quantize_weight("wb", 0)
+        pick_words(1, {})
+        round_weight("wb", 1, on_scalar)
+        quantize_weight("wb", 1)
+        pick_scales(1, {"dst": "dst_picked1", "src": "src_picked1"})
+        round_weight("wo", 0, on_scalar)
+        round_weight("wo", 1, [(nc.scalar.copy, 0, N // 2), (nc.vector.tensor_copy, N // 2, N)])
         edge_weight = held([P, J], F32, "edge_weight", "table_scales")
         nc.sync.dma_start(edge_weight[:], wgo)
-        identity = held([P, P], F32, "identity", "wb_grouped0_0")
-        make_identity(nc, identity[:])
-        for b, banks in enumerate(("AC", "BD", "EG", "FH")):
-            gate_products(b, banks)
         for b in range(4):
-            gate(b)
-        round_weight("wo", 1, N // 2, N, nc.vector.tensor_copy, "")
-        quantize_weight("wo", 0, [(0, N)], "")
-        quantize_weight("wo", 1, [(0, N // 2), (N // 2, N)], "")
-        pick_words(512, 768, {"dst": "wb_grouped1_0", "src": "wb_raw1_0"})
-        own_products((0, 1), "AB")
-        gate_products(4, "EC")
+            gate_products(b)
+        gate(0, "wo_raw0")
+        gate(1, "wo_raw1")
+        gate(2)
+        gate(3)
+        for a in range(PASSES):
+            quantize_weight("wo", a)
+        pick_words(2, {"dst": "wb_grouped1", "src": "wb_raw1"})
+
+        own_products((0, 1), ("za0", "za1"))
+        gate_products(4, "za2", "ms0")
         gate(4)
-        finish((0, 1), "AB")
-        pick_words(768, J, {"src": "eta2", "dst": "eta3"})
+        finish((0, 1), ("ow0", "ow1"))
+        pick_words(3, {"src": "eta2", "dst": "eta3"})
         for t in range(PACK):
-            scatter(t, 0, 256)
-        for b, banks in ((5, "FD"), (6, "EG")):
-            gate_products(b, banks)
-            gate(b)
-        own_products((2, 3), "HC")
-        finish((2, 3), "AB")
-        for t in range(3):
-            scatter(t, 256, 512)
-        gate_products(7, "FH")
-        gate(7)
-        own_products((4, 5), "CA")
-        finish((4, 5), "BF")
+            scatter(t, 0, 0)
+        gate_products(5, "za3", "ms1")
+        gate(5)
+        gate_products(6, "za4", "ms2")
+        gate(6, "eta2")
+        own_products((2, 3), ("ms3", "ms4"))
+        finish((2, 3), ("turned0", "turned1"))
+        for t in (0, 1, 2):
+            scatter(t, 1, 1)
+        gate_products(7, "za5", "ow2")
+        gate(7, "eta3")
+        own_products((4, 5), ("ow3", "turned2"))
+        finish((4, 5), ("turned3", "za7"))
         for t in (0, 1):
-            scatter(t, 512, 768)
-        own_products((6, 7), "CA")
-        finish((6, 7), "DG")
-        for t in (0, 1):
-            scatter(t, 768, J)
+            scatter(t, 2, 2)
+        own_products((6, 7), ("ow4", "ow5"))
+        finish((6, 7), ("ms5", "ms6"))
+        for t, first_quarter in enumerate((3, 3, 2, 1)):
+            scatter(t, first_quarter, 3)
             page_done(t)
-        scatter(2, 512, J)
-        page_done(2)
-        scatter(3, 256, J)
-        nc.sync.dma_start(out_rows[3], pages[3][:])
 
         out_codes = held([P, T], U32, "out_codes")
         out_plane = held([P, T], U8, "out_plane")
@@ -309,16 +307,18 @@ def tile_list_rgg_ownreluP_kernel(
                 cols = slice((c - 1) * CHUNK, (c + 1) * CHUNK)
                 nc.sync.dma_start(code_rows[:, cols], out_codes[:, cols].bitcast(I32))
 
-        for c in range(CHUNKS):
-            round_page(3, c, nc.vector.tensor_copy if c < 2 else nc.scalar.copy)
-        for c in range(CHUNKS - 3, CHUNKS):
+        vector_weaves = CHUNKS - SCALAR_WEAVES
+        for c in range(vector_weaves, CHUNKS):
             weave(c, nc.scalar.copy)
         weave(0, nc.vector.tensor_copy)
         for c in range(CHUNKS):
-            if c + 1 < CHUNKS - 3:
+            if c + 1 < vector_weaves:
                 weave(c + 1, nc.vector.tensor_copy)
             quantize_out(c)
         plane_rows = out_2[0].bitcast(I32)
-        for q in range(4):
+        for q in range(P // QUADRANT):
             queue = nc.sync if q % 2 == 0 else nc.scalar
-            queue.dma_start(plane_rows[4 * q : 4 * q + 4, :], out_plane[32 * q : 32 * q + 4, :].bitcast(I32))
+            queue.dma_start(
+                plane_rows[PLANE_ROWS * q : PLANE_ROWS * (q + 1), :],
+                out_plane[QUADRANT * q : QUADRANT * q + PLANE_ROWS, :].bitcast(I32),
+            )

from contextlib import ExitStack

import concourse.mybir as mybir
from concourse.masks import make_identity

K, N, T, J = 1024, 512, 2048, 1024
FLOPS = 4 * 2 * K * N * J

F32 = mybir.dt.float32
BF16 = mybir.dt.bfloat16
I32 = mybir.dt.int32
U32 = mybir.dt.uint32
U16 = mybir.dt.uint16
U8 = mybir.dt.uint8
FP8X4 = mybir.dt.float8_e4m3fn_x4
FP4X4 = mybir.dt.float4_e2m1fn_x4
ACT = mybir.ActivationFunctionType
MULT = mybir.AluOpType.mult

P = 128
PACK = 4
PASSES = K // (P * PACK)
LIST_ROWS = 16
QUADRANT = 32
PLANE_ROWS = 4
SECOND_PASS_ROW = 16
LINE = 4
BLOCK = 128
QUARTER = J // 4
HALF = J // 2
CHUNK = 256
CHUNKS = T // CHUNK
VECTOR_ROUNDS = 2
SCALAR_WEAVES = 3


def tile_list_rgg_ownreluP_kernel(
    tc, tab_words, tab_scales, wa_words, wa_scales, wb, wc_words, wc_scales, wo, wgo, offs, offs2, out_0, out_1, out_2
):
    nc = tc.nc
    with ExitStack() as ctx:
        keep = ctx.enter_context(tc.tile_pool(name="keep", bufs=1))
        ring = ctx.enter_context(tc.tile_pool(name="ring", bufs=2))
        psum = ctx.enter_context(tc.psum_pool(name="psum", bufs=1))

        def held(shape, dtype, name, slot=""):
            return keep.tile(shape, dtype, name=name, tag=slot or name, align_bytes=64)

        src_list = keep.tile([P, J // LIST_ROWS], U16, name="src_list")
        dst_list = keep.tile([P, J // LIST_ROWS], U16, name="dst_list")
        nc.sync.dma_start(src_list[:], offs)
        nc.sync.dma_start(dst_list[:], offs2)
        lists = {"src": src_list, "dst": dst_list}

        def entries(name, first, last):
            return lists[name][:, first // LIST_ROWS : last // LIST_ROWS]

        table_scales = held([P, T], U8, "table_scales")
        nc.gpsimd.memset(table_scales[:].bitcast(I32), 0)
        weight_planes = held([P, 2 * PASSES * N], U8, "weight_planes")
        nc.vector.memset(weight_planes[:].bitcast(I32), 0)
        packed_words, packed_scales = {}, {}
        for i, name in enumerate(("wa", "wc")):
            packed_words[name] = held([P, PASSES * 2 * N], U8, name + "_words")
            packed_scales[name] = weight_planes[:, i * PASSES * N : (i + 1) * PASSES * N]
        moved_planes = held([P, 2 * J], U8, "moved_planes")
        nc.vector.memset(moved_planes[:].bitcast(I32), 0)
        moved_scales = {}
        for i, key in enumerate((name, h) for h in range(2) for name in ("dst", "src")):
            moved_scales[key] = moved_planes[:, i * HALF : (i + 1) * HALF]
        identity = held([P, P], F32, "identity")
        make_identity(nc, identity[:])

        def load_packed_words(name, words):
            nc.sync.dma_start(
                packed_words[name][:].bitcast(I32).rearrange("p (a c) -> p a c", a=PASSES),
                words.rearrange("a p c -> p a c").bitcast(I32),
            )

        def load_packed_scales(name, scales):
            rows = scales.rearrange("a (q r) n -> r q a n", r=PLANE_ROWS)
            for r in range(PLANE_ROWS):
                nc.sync.dma_start(
                    packed_scales[name][r:P:QUADRANT, :].bitcast(I32).rearrange("q (a c) -> q a c", a=PASSES),
                    rows[r].bitcast(I32),
                )

        raw = {}

        def load_raw(name, w, a):
            raw[name, a] = held([P, PACK, N], F32, "%s_raw%d" % (name, a))
            rows = w[a * P * PACK : (a + 1) * P * PACK, :]
            nc.sync.dma_start(raw[name, a][:], rows.rearrange("(p i) n -> p i n", i=PACK))

        scale_rows = tab_scales.rearrange("a (q r) t -> r q a t", r=PLANE_ROWS)
        for r in range(PLANE_ROWS):
            nc.sync.dma_start(table_scales[r:P:SECOND_PASS_ROW, :].bitcast(I32), scale_rows[r].bitcast(I32))
        load_raw("wb", wb, 0)
        load_packed_words("wa", wa_words)
        load_packed_words("wc", wc_words)
        table_words = held([P, T], I32, "table_words")
        nc.sync.dma_start(table_words[:], tab_words[0].rearrange("p t b -> p (t b)").bitcast(I32))
        load_packed_scales("wa", wa_scales)
        load_raw("wb", wb, 1)
        load_packed_scales("wc", wc_scales)
        load_raw("wo", wo, 0)
        load_raw("wo", wo, 1)

        pages = [held([P, T], F32, "page%d" % t) for t in range(PACK)]
        for t in range(PACK):
            nc.vector.memset(pages[t][:].bitcast(I32), 0)

        picked_scales, parted = {}, {}

        def pick_scales(h, slots):
            for name in ("dst", "src"):
                picked_scales[name, h] = held([P, HALF], U8, "%s_picked_scales%d" % (name, h), slots.get(name, ""))
                nc.vector.tensor_copy(
                    picked_scales[name, h][:], table_scales[:].indirect(entries(name, h * HALF, (h + 1) * HALF))
                )
                nc.sync.dma_start(
                    moved_scales[name, h][0 : P - SECOND_PASS_ROW, :].bitcast(I32),
                    picked_scales[name, h][SECOND_PASS_ROW:P, :].bitcast(I32),
                )

        def pick_words(q, slots):
            picked = {}
            for name in ("dst", "src"):
                picked[name] = held([P, QUARTER], U32, "%s_picked%d" % (name, q), slots.get(name, ""))
                nc.vector.tensor_copy(
                    picked[name][:], table_words[:].bitcast(U32).indirect(entries(name, q * QUARTER, (q + 1) * QUARTER))
                )
            for name in ("dst", "src"):
                parted[name, q] = held([P, PASSES * 2 * QUARTER], U8, "%s_parted%d" % (name, q))
                nc.vector.tensor_copy(
                    parted[name, q][:].bitcast(U16).rearrange("p (a j) -> p a j", a=PASSES),
                    picked[name][:].bitcast(U16).rearrange("p (j a) -> p a j", a=PASSES),
                )

        grouped, codes, planes = {}, {}, {}

        def round_weight(name, a, shares):
            grouped[name, a] = held([P, N * PACK], BF16, "%s_grouped%d" % (name, a))
            for copy, first, last in shares:
                copy(
                    grouped[name, a][:, first * PACK : last * PACK].rearrange("p (c m i) -> p c i m", m=LINE, i=PACK),
                    raw[name, a][:, :, first:last].rearrange("p i (c m) -> p c i m", m=LINE),
                )

        def quantize_weight(name, a):
            codes[name, a] = held([P, N], U32, "%s_codes%d" % (name, a))
            planes[name, a] = held([P, N], U8, "%s_plane%d" % (name, a))
            nc.vector.quantize_mx(codes[name, a][:].bitcast(FP8X4), planes[name, a][:], grouped[name, a][:])

        def moving(name, a):
            if name in packed_words:
                return (
                    packed_words[name][:, a * 2 * N : (a + 1) * 2 * N].bitcast(FP4X4),
                    packed_scales[name][:, a * N : (a + 1) * N],
                )
            return codes[name, a][:].bitcast(FP8X4), planes[name, a][:]

        def stationary(name, a, b):
            q, in_quarter = divmod(b * BLOCK, QUARTER)
            h, in_half = divmod(b * BLOCK, HALF)
            at = 2 * (a * QUARTER + in_quarter)
            plane = picked_scales[name, h] if a == 0 else moved_scales[name, h]
            return parted[name, q][:, at : at + 2 * BLOCK].bitcast(FP4X4), plane[:, in_half : in_half + BLOCK]

        sums, bank_tags = {}, {}

        def bank(name, after=""):
            bank_tags[name] = bank_tags[after] if after else name
            sums[name] = psum.tile([P, N], F32, name=name, tag=bank_tags[name])
            return sums[name]

        def product(result_bank, terms, b):
            steps = [(w, v, a) for a in range(PASSES) for w, v in terms]
            for s, (w, v, a) in enumerate(steps):
                lhs, lhs_scale = stationary(v, a, b)
                rhs, rhs_scale = moving(w, a)
                nc.tensor.matmul_mx(
                    result_bank[:], lhsT=lhs, lhsT_scale=lhs_scale, rhs=rhs, rhs_scale=rhs_scale,
                    start=(s == 0), stop=(s == len(steps) - 1),
                )

        def dealt(name):
            return sums[name][:].rearrange("p (m t) -> p t m", t=PACK)

        def gate_products(b, za_after="", ms_after=""):
            product(bank("za%d" % b, za_after), [("wa", "dst"), ("wb", "src")], b)
            product(bank("ms%d" % b, ms_after), [("wc", "src")], b)

        messages = {}

        def gate(b, slot=""):
            eta = held([P, PACK, P], F32, "eta%d" % b, slot)
            nc.scalar.activation(eta[:], dealt("za%d" % b), ACT.Sigmoid)
            messages[b] = held([P, PACK, P], F32, "message%d" % b)
            nc.vector.tensor_tensor(messages[b][:], dealt("ms%d" % b), eta[:], MULT)

        def own_products(blocks, afters):
            for b, after in zip(blocks, afters):
                product(bank("ow%d" % b, after), [("wo", "dst")], b)

        result = held([P, PACK, J], F32, "result")

        def finish(blocks, afters):
            own = {}
            for b in blocks:
                own[b] = ring.tile([P, PACK, P], F32, name="own")
                nc.scalar.copy(own[b][:], dealt("ow%d" % b))
            for b, after in zip(blocks, afters):
                turned = bank("turned%d" % b, after)
                for t in range(PACK):
                    cols = slice(t * BLOCK, (t + 1) * BLOCK)
                    nc.tensor.matmul(
                        turned[:, cols], own[b][:, t, :], identity[:], start=True, stop=False, is_transpose=True
                    )
                    nc.tensor.matmul(
                        turned[:, cols], messages[b][:, t, :], identity[:], start=False, stop=True, is_transpose=True
                    )
                nc.scalar.activation(
                    result[:, :, b * BLOCK : (b + 1) * BLOCK], turned[:].rearrange("p (t j) -> p t j", t=PACK), ACT.Relu
                )

        def scatter(t, first_quarter, last_quarter):
            first, last = first_quarter * QUARTER, (last_quarter + 1) * QUARTER
            nc.vector.tensor_tensor(
                pages[t][:].indirect(entries("dst", first, last)), result[:, t, first:last], edge_weight[:, first:last], MULT
            )

        pairs = [held([P, 2, CHUNK, 2], BF16, "pairs%d" % c) for c in range(CHUNKS)]
        out_rows = out_0.rearrange("(p t) c -> t p c", t=PACK)

        def page_done(t):
            nc.sync.dma_start(out_rows[t], pages[t][:])
            for c in range(CHUNKS):
                copy = nc.vector.tensor_copy if t >= 2 and c < VECTOR_ROUNDS else nc.scalar.copy
                copy(pairs[c][:, t // 2, :, t % 2], pages[t][:, c * CHUNK : (c + 1) * CHUNK])

        on_scalar = [(nc.scalar.copy, 0, N)]
        round_weight("wb", 0, on_scalar)
        pick_scales(0, {})
        pick_words(0, {})
        quantize_weight("wb", 0)
        pick_words(1, {})
        round_weight("wb", 1, on_scalar)
        quantize_weight("wb", 1)
        pick_scales(1, {"dst": "dst_picked1", "src": "src_picked1"})
        round_weight("wo", 0, on_scalar)
        round_weight("wo", 1, [(nc.scalar.copy, 0, N // 2), (nc.vector.tensor_copy, N // 2, N)])
        edge_weight = held([P, J], F32, "edge_weight", "table_scales")
        nc.sync.dma_start(edge_weight[:], wgo)
        for b in range(4):
            gate_products(b)
        gate(0, "wo_raw0")
        gate(1, "wo_raw1")
        gate(2)
        gate(3)
        for a in range(PASSES):
            quantize_weight("wo", a)
        pick_words(2, {"dst": "wb_grouped1", "src": "wb_raw1"})

        own_products((0, 1), ("za0", "za1"))
        gate_products(4, "za2", "ms0")
        gate(4)
        finish((0, 1), ("ow0", "ow1"))
        pick_words(3, {"src": "eta2", "dst": "eta3"})
        for t in range(PACK):
            scatter(t, 0, 0)
        gate_products(5, "za3", "ms1")
        gate(5)
        gate_products(6, "za4", "ms2")
        gate(6, "eta2")
        own_products((2, 3), ("ms3", "ms4"))
        finish((2, 3), ("turned0", "turned1"))
        for t in (0, 1, 2):
            scatter(t, 1, 1)
        gate_products(7, "za5", "ow2")
        gate(7, "eta3")
        own_products((4, 5), ("ow3", "turned2"))
        finish((4, 5), ("turned3", "za7"))
        for t in (0, 1):
            scatter(t, 2, 2)
        own_products((6, 7), ("ow4", "ow5"))
        finish((6, 7), ("ms5", "ms6"))
        for t, first_quarter in enumerate((3, 3, 2, 1)):
            scatter(t, first_quarter, 3)
            page_done(t)

        out_codes = held([P, T], U32, "out_codes")
        out_plane = held([P, T], U8, "out_plane")
        code_rows = out_1[0].rearrange("p t b -> p (t b)").bitcast(I32)
        woven = [held([P, CHUNK * PACK], BF16, "woven%d" % c) for c in range(CHUNKS)]

        def weave(c, copy):
            copy(
                woven[c][:].bitcast(F32).rearrange("p (c u) -> p c u", u=2),
                pairs[c][:].rearrange("p u c e -> p u (c e)").bitcast(F32).rearrange("p u c -> p c u"),
            )

        def quantize_out(c):
            cols = slice(c * CHUNK, (c + 1) * CHUNK)
            nc.vector.quantize_mx(out_codes[:, cols].bitcast(FP8X4), out_plane[:, cols], woven[c][:])
            if c % 2 == 1:
                cols = slice((c - 1) * CHUNK, (c + 1) * CHUNK)
                nc.sync.dma_start(code_rows[:, cols], out_codes[:, cols].bitcast(I32))

        vector_weaves = CHUNKS - SCALAR_WEAVES
        for c in range(vector_weaves, CHUNKS):
            weave(c, nc.scalar.copy)
        weave(0, nc.vector.tensor_copy)
        for c in range(CHUNKS):
            if c + 1 < vector_weaves:
                weave(c + 1, nc.vector.tensor_copy)
            quantize_out(c)
        plane_rows = out_2[0].bitcast(I32)
        for q in range(P // QUADRANT):
            queue = nc.sync if q % 2 == 0 else nc.scalar
            queue.dma_start(
                plane_rows[PLANE_ROWS * q : PLANE_ROWS * (q + 1), :],
                out_plane[QUADRANT * q : QUADRANT * q + PLANE_ROWS, :].bitcast(I32),
            )
